import numpy as np
import ml_dtypes


def mxq(x, axis, fmt="e4m3"):
    dtype, down = {"e4m3": (ml_dtypes.float8_e4m3fn, 7), "e5m2": (ml_dtypes.float8_e5m2, 14)}[fmt]
    v = np.moveaxis(np.asarray(x, np.float32).astype(ml_dtypes.bfloat16).astype(np.float64), axis, -1)
    blocks = v.reshape(v.shape[:-1] + (-1, 32))
    amax = np.abs(blocks).max(-1, keepdims=True)
    byte = np.maximum(np.where(amax > 0, np.frexp(amax)[1] - 1 + 127, 0) - down, 1)
    scale = np.exp2(byte - 127.0)
    codes = (blocks / scale).astype(np.float32).astype(dtype).astype(np.float64)
    return np.moveaxis((codes * scale).reshape(v.shape), -1, axis)


WIDE = False


def mx_kscale(k):
    if not WIDE:
        return np.ones(k)
    levels = np.array([10, -10, 5, -5, 0])
    if k % 512:
        return np.exp2(np.random.permutation(np.resize(levels, k // 32))).repeat(32)
    a = np.empty((k // 512, 16))
    for p in range(k // 512):
        a[p, :8] = np.random.permutation(np.resize(levels, 8))
        for g in range(8):
            far = levels[np.abs(levels - a[p, g]) >= 10]
            a[p, g + 8] = far[np.random.randint(len(far))]
    return np.exp2(a.ravel()).repeat(32)


def f64(x):
    return np.asarray(x).astype(np.float64)


def striped(idx):
    return np.tile(idx.reshape(-1, 16).T, (8, 1)).astype(np.uint16)


def unstriped(offs):
    return offs[:16].T.reshape(-1).astype(np.int64)


def striped8(idx):
    return np.concatenate([x.reshape(-1, 16).T for x in idx]).astype(np.uint16)


def runs(offs, k):
    lists = np.stack([offs[16 * r : 16 * r + 16].T.reshape(-1) for r in range(8)]).astype(np.int64)
    return lists[np.arange(k) % 512 // 64]


def pack_weight(w):
    k, n = w.shape
    w = f64(np.asarray(w, np.float32).astype(ml_dtypes.bfloat16)).reshape(k // 32, 32, n)
    amax = np.abs(w).max(1)
    byte = np.clip(np.where(amax > 0, np.frexp(amax)[1] - 1 + 127 - 7, 1), 1, 254)
    scaled = (w * np.exp2(127.0 - byte)[:, None, :]).reshape(k, n).astype(np.float32)
    words = np.ascontiguousarray(scaled.reshape(k // 512, 128, 4, n).transpose(0, 1, 3, 2)).astype(ml_dtypes.float8_e4m3fn).view(np.uint8)
    return words, np.ascontiguousarray(byte.astype(np.uint8).reshape(k // 512, 16, n))


def unpack_weight(words, scales):
    g, p, n, _ = words.shape
    vals = np.ascontiguousarray(words).view(ml_dtypes.float8_e4m3fn).astype(np.float64) * np.repeat(np.exp2(scales.astype(np.float64) - 127.0), 8, axis=1)[..., None]
    return vals.transpose(0, 1, 3, 2).reshape(g * 512, n)


E2M1 = np.array([0.0, 0.5, 1.0, 1.5, 2.0, 3.0, 4.0, 6.0, -0.0, -0.5, -1.0, -1.5, -2.0, -3.0, -4.0, -6.0])


def pack_fp4(w):
    k, n = w.shape
    w = f64(np.asarray(w, np.float32).astype(ml_dtypes.bfloat16)).reshape(k // 32, 32, n)
    amax = np.abs(w).max(1)
    mant, ex = np.frexp(amax / 6.0)
    byte = np.clip(np.where(amax > 0, np.where(mant > 0.5, ex, ex - 1) + 127, 1), 1, 254)
    scaled = (w * np.exp2(127.0 - byte)[:, None, :]).reshape(k, n).astype(np.float32)
    c = np.ascontiguousarray(scaled.reshape(k // 512, 128, 4, n).transpose(0, 1, 3, 2)).astype(ml_dtypes.float4_e2m1fn).view(np.uint8) & 0xF
    words = (c[..., 0::2] | (c[..., 1::2] << 4)).reshape(k // 512, 128, 2 * n)
    return np.ascontiguousarray(words), np.ascontiguousarray(byte.astype(np.uint8).reshape(k // 512, 16, n))


def unpack_fp4(words, scales):
    g, _, n = scales.shape
    words = np.ascontiguousarray(words).reshape(g, 128, n, 2)
    nib = np.empty((g, 128, n, 4), np.uint8)
    nib[..., 0::2] = words & 0xF
    nib[..., 1::2] = words >> 4
    vals = E2M1[nib] * np.repeat(np.exp2(scales.astype(np.float64) - 127.0), 8, axis=1)[..., None]
    return vals.transpose(0, 1, 3, 2).reshape(g * 512, n)


def planes(y):
    n, m = y.shape
    v = y.astype(np.float32).astype(ml_dtypes.bfloat16).astype(np.float64).reshape(n // 32, 32, m)
    top = np.abs(v).max(1)
    byte = np.clip(np.where(top > 0, np.frexp(top)[1] - 1 + 127 - 7, 1), 1, 254)
    codes = (v * np.exp2(127.0 - byte)[:, None, :]).reshape(n, m).astype(np.float32).astype(ml_dtypes.float8_e4m3fn).view(np.uint8)
    words = codes.reshape(n // 512, 128, 4, m).transpose(0, 1, 3, 2)
    return np.ascontiguousarray(words), np.ascontiguousarray(byte.astype(np.uint8).reshape(n // 512, 16, m))


K, T, S, N, H, W = 512, 2048, 512, 512, 512, 256


def setup_inputs():
    n = np.random.standard_normal
    s = mx_kscale(K)[:, None]
    u = mx_kscale(H)
    packed_xT = pack_weight(n((K, T)) * s)
    packed_w1 = pack_fp4(n((K, H)) / np.sqrt(K) / s)
    packed_w2 = pack_fp4(n((H, N)) / np.sqrt(H) / u[:, None])
    perm = np.stack([np.random.permutation(S) for _ in range(8)])
    return {
        "x_words": packed_xT[0],
        "x_scales": packed_xT[1],
        "w1_words": packed_w1[0],
        "w1_scales": packed_w1[1],
        "gn": (np.random.uniform(0.5, 1.5, (H, 1)) * u[:, None]).astype(np.float32),
        "w2_words": packed_w2[0],
        "w2_scales": packed_w2[1],
        "offs": striped(np.random.permutation(T)[:S]),
        "n1": striped8(perm[:, :W]),
        "n2": striped8(perm[:, W:]),
        "n3": striped8(np.stack([np.random.permutation(S) for _ in range(8)])),
        "n4": striped8(np.stack([np.random.permutation(S) for _ in range(8)])),
        "n5": striped8(np.stack([np.random.permutation(S) for _ in range(8)])),
        "n6": striped8(np.stack([np.random.permutation(S) for _ in range(8)])),
    }


def reference(x_words, x_scales, w1_words, w1_scales, gn, w2_words, w2_scales, offs, n1, n2, n3, n4, n5, n6):
    xq = unpack_weight(x_words, x_scales)[:, unstriped(offs)]
    y = unpack_fp4(w1_words, w1_scales).T @ xq
    pb = y[np.arange(H)[:, None], runs(n2, H)]
    pa = y[np.arange(H)[:, None], runs(n1, H)]
    rb = pb - (0.5 * pa)
    ra = np.sqrt((pa) ** 2 + (pb) ** 2 + 0.25)
    ds = np.zeros((H, S))
    ds[np.arange(H)[:, None], runs(n1, H)] = ra
    dt = ds.copy()
    dt[np.arange(H)[:, None], runs(n2, H)] = rb
    z = f64(gn) * dt
    h = unpack_fp4(w2_words, w2_scales).T @ mxq(z, 0, "e4m3")
    out_0 = np.maximum(h[np.arange(N)[:, None], runs(n3, N)] + y[np.arange(H)[:, None], runs(n5, H)], h[np.arange(N)[:, None], runs(n4, N)] + y[np.arange(H)[:, None], runs(n6, H)])
    return (out_0,) + planes(out_0)

@@ -1,0 +1,182 @@
+from contextlib import ExitStack
+
+import concourse.mybir as mybir
+
+K, T, S, N, H, W = 512, 2048, 512, 512, 512, 256
+FLOPS = 2 * K * H * S + 2 * H * N * S
+
+F32 = mybir.dt.float32
+BF16 = mybir.dt.bfloat16
+I32 = mybir.dt.int32
+U32 = mybir.dt.uint32
+U16 = mybir.dt.uint16
+U8 = mybir.dt.uint8
+FP8X4 = mybir.dt.float8_e4m3fn_x4
+FP4X4 = mybir.dt.float4_e2m1fn_x4
+ALU = mybir.AluOpType
+ACT = mybir.ActivationFunctionType
+
+P = 128
+PACK = 4
+QUADS = 4
+PER_COL = 16
+PIECES = ((0, 256), (256, 384), (384, 512))
+
+
+def tile_picked_skippathbpolar_none_po_kernel(
+    tc, x_words, x_scales, w1_words, w1_scales, gn, w2_words, w2_scales,
+    offs, n1, n2, n3, n4, n5, n6, out_0, out_1, out_2,
+):
+    nc = tc.nc
+    with ExitStack() as ctx:
+        lists = ctx.enter_context(tc.tile_pool(name="lists", bufs=1))
+        sb = ctx.enter_context(tc.tile_pool(name="sb", bufs=1))
+        psum = ctx.enter_context(tc.psum_pool(name="psum", bufs=1))
+
+        def list_tile(src, name):
+            tile = lists.tile(list(src.shape), U16, name=name)
+            nc.sync.dma_start(tile[:], src)
+            return tile
+
+        def scale_tile(width, name):
+            tile = sb.tile([P, width], U8, name=name, align_bytes=64)
+            nc.vector.memset(tile[:].bitcast(I32), 0)
+            return tile
+
+        def load_scale_rows(tile, src):
+            for q in range(QUADS):
+                nc.sync.dma_start(tile[32 * q : 32 * q + 4, :].bitcast(I32), src[0, 4 * q : 4 * q + 4, :].bitcast(I32))
+
+        def deal(raw, name, b):
+            dealt = sb.tile([P, PACK, P * b], U8, name=name, align_bytes=64)
+            nc.vector.tensor_copy(
+                dealt[:].rearrange("p t (m b) -> p t m b", b=b),
+                raw[:].rearrange("p (m t b) -> p t m b", t=PACK, b=b),
+            )
+            return dealt
+
+        def interleave(engine_copy, dst, src):
+            engine_copy(
+                dst.rearrange("p (c i t) -> p c t i", i=4, t=PACK),
+                src.rearrange("p t (c i) -> p c t i", i=4),
+            )
+
+        xs = scale_tile(T, "xs")
+        w1s_raw = scale_tile(H, "w1s_raw")
+        w2s_raw = scale_tile(N, "w2s_raw")
+        y = [sb.tile([P, 2 * S], F32, name=f"y{t}") for t in range(PACK)]
+        for t in range(PACK):
+            nc.vector.memset(y[t][:, S:], 0.0)
+
+        xw = sb.tile([P, T], I32, name="xw")
+        nc.scalar.dma_start(xw[:], x_words[0].rearrange("p c r -> p (c r)").bitcast(I32))
+        w1w_raw = sb.tile([P, 2 * H], U8, name="w1w_raw")
+        nc.sync.dma_start(w1w_raw[:].bitcast(I32), w1_words[0].bitcast(I32))
+        load_scale_rows(xs, x_scales)
+        l_offs = list_tile(offs, "l_offs")
+        load_scale_rows(w1s_raw, w1_scales)
+        l1 = list_tile(n1, "l1")
+        l2 = list_tile(n2, "l2")
+        w2w_raw = sb.tile([P, 2 * N], U8, name="w2w_raw")
+        nc.sync.dma_start(w2w_raw[:].bitcast(I32), w2_words[0].bitcast(I32))
+        load_scale_rows(w2s_raw, w2_scales)
+        gain = sb.tile([P, PACK], F32, name="gain")
+        nc.sync.dma_start(gain[:], gn.rearrange("(p t) o -> p (t o)", t=PACK))
+        l5 = list_tile(n5, "l5")
+        l6 = list_tile(n6, "l6")
+        l3 = list_tile(n3, "l3")
+        l4 = list_tile(n4, "l4")
+
+        w1w = deal(w1w_raw, "w1w", 2)
+        gs = sb.tile([P, S], U8, name="gs", align_bytes=64)
+        nc.vector.tensor_copy(gs[:], xs[:].indirect(l_offs[:]))
+        w1s = deal(w1s_raw, "w1s", 1)
+        gw = sb.tile([P, S], U32, name="gw", align_bytes=64)
+        for c0 in (0, S // 2):
+            nc.vector.tensor_copy(
+                gw[:, c0 : c0 + S // 2],
+                xw[:].bitcast(U32).indirect(l_offs[:, c0 // PER_COL : (c0 + S // 2) // PER_COL]),
+            )
+
+        def product(ww, ws, t, codes, scales, c0, c1, dst, tag):
+            acc = psum.tile([P, c1 - c0], F32, name=tag, tag=tag)
+            nc.tensor.matmul_mx(
+                out=acc[:], lhsT=ww[:, t, :].bitcast(FP4X4), lhsT_scale=ws[:, t, :],
+                rhs=codes[:, c0:c1].bitcast(FP8X4), rhs_scale=scales[:, c0:c1], start=True, stop=True,
+            )
+            nc.scalar.copy(dst[:, c0:c1], acc[:])
+
+        product(w1w, w1s, 0, gw, gs, 0, S // 2, y[0], "bank4")
+        product(w1w, w1s, 0, gw, gs, S // 2, S, y[0], "bank0")
+        for t in range(1, PACK):
+            product(w1w, w1s, t, gw, gs, 0, S, y[t], f"bank{t}")
+
+        w2w = deal(w2w_raw, "w2w", 2)
+        w2s = deal(w2s_raw, "w2s", 1)
+
+        pa = sb.tile([P, PACK, W], F32, name="pa")
+        pb = sb.tile([P, PACK, W], F32, name="pb")
+        sa = sb.tile([P, PACK, W], F32, name="sa")
+        sq = sb.tile([P, PACK, W], F32, name="sq")
+        ssum = sb.tile([P, PACK, W], F32, name="ssum")
+        for t in range(PACK):
+            nc.vector.tensor_scalar(pa[:, t, :], y[t][:].indirect(l1[:]), -0.5, 0.0, ALU.mult, ALU.add)
+            nc.vector.tensor_copy(pb[:, t, :], y[t][:].indirect(l2[:]))
+            nc.scalar.activation(sa[:, t, :], pa[:, t, :], ACT.Square, scale=2.0)
+            nc.scalar.activation(sq[:, t, :], pb[:, t, :], ACT.Square)
+
+        dt = [sb.tile([P, S], F32, name=f"dt{t}") for t in range(PACK)]
+        ra = []
+        for half in range(2):
+            ts = slice(2 * half, 2 * half + 2)
+            for t in range(2 * half, 2 * half + 2):
+                nc.vector.tensor_tensor(dt[t][:].indirect(l2[:]), pb[:, t, :], pa[:, t, :], ALU.add)
+            nc.vector.tensor_tensor(ssum[:, ts, :], sa[:, ts, :], sq[:, ts, :], ALU.add)
+            root = sb.tile([P, 2, W], F32, name=f"ra{half}", tag=f"ra{half}", align_bytes=64)
+            nc.scalar.activation(root[:], ssum[:, ts, :], ACT.Sqrt, bias=0.25)
+            ra.append(root)
+
+        zp = sb.tile([P, PACK, S], BF16, name="zp")
+        for t in range(PACK):
+            nc.vector.tensor_copy(dt[t][:].indirect(l1[:]), ra[t // 2][:, t % 2, :])
+            nc.scalar.activation(zp[:, t, :], dt[t][:], ACT.Copy, scale=gain[:, t : t + 1])
+        zq = sb.tile([P, PACK * S], BF16, name="zq", tag="zq", align_bytes=64)
+        interleave(nc.scalar.copy, zq[:], zp[:])
+
+        y5 = sb.tile([P, PACK, S], F32, name="y5", tag="ra1", align_bytes=64)
+        for t in range(PACK):
+            nc.vector.tensor_copy(y5[:, t, :], y[t][:].indirect(l5[:]))
+
+        zw = sb.tile([P, S], U32, name="zw", align_bytes=64)
+        zs = sb.tile([P, S], U8, name="zs", align_bytes=64)
+        nc.vector.quantize_mx(out=zw[:].bitcast(FP8X4), scales=zs[:], in_=zq[:])
+        h = [sb.tile([P, S], F32, name=f"h{t}") for t in range(PACK)]
+        for t in range(PACK):
+            product(w2w, w2s, t, zw, zs, 0, S, h[t], f"bank{t}")
+
+        y6 = sb.tile([P, PACK, S], F32, name="y6", tag="zq", align_bytes=64)
+        for t in range(PACK):
+            nc.vector.tensor_copy(y6[:, t, :], y[t][:].indirect(l6[:]))
+
+        ow = sb.tile([P, S], I32, name="ow", align_bytes=64)
+        osc = sb.tile([P, S], U8, name="osc", align_bytes=64)
+        out_rows = out_0.rearrange("(p t) j -> p t j", t=PACK)
+        out_words = out_1[0].rearrange("p c r -> p (c r)").bitcast(I32)
+        for c0, c1 in PIECES:
+            w = c1 - c0
+            lc = slice(c0 // PER_COL, c1 // PER_COL)
+            left = sb.tile([P, PACK, w], F32, name=f"left{c0}")
+            right = sb.tile([P, PACK, w], F32, name=f"right{c0}")
+            for t in range(PACK):
+                nc.vector.tensor_tensor(left[:, t, :], h[t][:].indirect(l3[:, lc]), y5[:, t, c0:c1], ALU.add)
+                nc.vector.tensor_tensor(right[:, t, :], h[t][:].indirect(l4[:, lc]), y6[:, t, c0:c1], ALU.add)
+            res = sb.tile([P, PACK, w], F32, name=f"res{c0}")
+            nc.vector.tensor_tensor(res[:], left[:], right[:], ALU.max)
+            nc.sync.dma_start(out_rows[:, :, c0:c1], res[:])
+            rq = sb.tile([P, PACK * w], BF16, name=f"rq{c0}", align_bytes=64)
+            interleave(nc.scalar.copy, rq[:], res[:])
+            nc.vector.quantize_mx(out=ow[:, c0:c1].bitcast(FP8X4), scales=osc[:, c0:c1], in_=rq[:])
+            nc.sync.dma_start(out_words[:, c0:c1], ow[:, c0:c1])
+        for q in range(QUADS):
+            queue = nc.scalar if q % 2 else nc.sync
+            queue.dma_start(out_2[0, 4 * q : 4 * q + 4, :].bitcast(I32), osc[32 * q : 32 * q + 4, :].bitcast(I32))

@@ -1,6 +1,7 @@
 from contextlib import ExitStack
 
 import concourse.mybir as mybir
+from concourse.masks import make_identity
 
 K, T, S, N, H, W = 512, 2048, 512, 512, 512, 256
 FLOPS = 2 * K * H * S + 2 * H * N * S
@@ -20,7 +21,7 @@ P = 128
 PACK = 4
 QUADS = 4
 PER_COL = 16
-PIECES = ((0, 256), (256, 384), (384, 512))
+BLOCKS = S // P
 
 
 def tile_picked_skippathbpolar_none_po_kernel(
@@ -43,15 +44,21 @@ def tile_picked_skippathbpolar_none_po_kernel(
             nc.vector.memset(tile[:].bitcast(I32), 0)
             return tile
 
-        def load_scale_rows(tile, src):
+        def load_scale_rows(tile, src, queues):
             for q in range(QUADS):
-                nc.sync.dma_start(tile[32 * q : 32 * q + 4, :].bitcast(I32), src[0, 4 * q : 4 * q + 4, :].bitcast(I32))
+                queues[q].dma_start(tile[32 * q : 32 * q + 4, :].bitcast(I32), src[0, 4 * q : 4 * q + 4, :].bitcast(I32))
+
+        def turn(dst, src, start, stop):
+            nc.tensor.matmul(dst, lhsT=src, rhs=ident[:], start=start, stop=stop, is_transpose=True)
+
+        def bank(index):
+            return psum.tile([P, PACK, P], F32, name=f"bank{index}", tag=f"bank{index}")
 
         def deal(raw, name, b):
             dealt = sb.tile([P, PACK, P * b], U8, name=name, align_bytes=64)
             nc.vector.tensor_copy(
-                dealt[:].rearrange("p t (m b) -> p t m b", b=b),
-                raw[:].rearrange("p (m t b) -> p t m b", t=PACK, b=b),
+                dealt[:].rearrange("p t (c i b) -> p c t i b", i=16 // b, b=b),
+                raw[:].rearrange("p (c i t b) -> p c t i b", i=16 // b, t=PACK, b=b),
             )
             return dealt
 
@@ -64,22 +71,22 @@ def tile_picked_skippathbpolar_none_po_kernel(
         xs = scale_tile(T, "xs")
         w1s_raw = scale_tile(H, "w1s_raw")
         w2s_raw = scale_tile(N, "w2s_raw")
-        y = [sb.tile([P, 2 * S], F32, name=f"y{t}") for t in range(PACK)]
-        for t in range(PACK):
-            nc.vector.memset(y[t][:, S:], 0.0)
+        y = [sb.tile([P, S], F32, name=f"y{t}") for t in range(PACK)]
+        ident = sb.tile([P, P], F32, name="ident")
+        make_identity(nc, ident[:])
 
-        xw = sb.tile([P, T], I32, name="xw")
-        nc.scalar.dma_start(xw[:], x_words[0].rearrange("p c r -> p (c r)").bitcast(I32))
         w1w_raw = sb.tile([P, 2 * H], U8, name="w1w_raw")
         nc.sync.dma_start(w1w_raw[:].bitcast(I32), w1_words[0].bitcast(I32))
-        load_scale_rows(xs, x_scales)
         l_offs = list_tile(offs, "l_offs")
-        load_scale_rows(w1s_raw, w1_scales)
-        l1 = list_tile(n1, "l1")
-        l2 = list_tile(n2, "l2")
+        load_scale_rows(xs, x_scales, (nc.sync, nc.sync, nc.scalar, nc.scalar))
+        xw = sb.tile([P, T], I32, name="xw")
+        nc.sync.dma_start(xw[:], x_words[0].rearrange("p c r -> p (c r)").bitcast(I32))
+        load_scale_rows(w1s_raw, w1_scales, (nc.sync,) * QUADS)
         w2w_raw = sb.tile([P, 2 * N], U8, name="w2w_raw")
         nc.sync.dma_start(w2w_raw[:].bitcast(I32), w2_words[0].bitcast(I32))
-        load_scale_rows(w2s_raw, w2_scales)
+        l1 = list_tile(n1, "l1")
+        l2 = list_tile(n2, "l2")
+        load_scale_rows(w2s_raw, w2_scales, (nc.sync,) * QUADS)
         gain = sb.tile([P, PACK], F32, name="gain")
         nc.sync.dma_start(gain[:], gn.rearrange("(p t) o -> p (t o)", t=PACK))
         l5 = list_tile(n5, "l5")
@@ -116,67 +123,135 @@ def tile_picked_skippathbpolar_none_po_kernel(
 
         pa = sb.tile([P, PACK, W], F32, name="pa")
         pb = sb.tile([P, PACK, W], F32, name="pb")
-        sa = sb.tile([P, PACK, W], F32, name="sa")
-        sq = sb.tile([P, PACK, W], F32, name="sq")
-        ssum = sb.tile([P, PACK, W], F32, name="ssum")
-        for t in range(PACK):
-            nc.vector.tensor_scalar(pa[:, t, :], y[t][:].indirect(l1[:]), -0.5, 0.0, ALU.mult, ALU.add)
-            nc.vector.tensor_copy(pb[:, t, :], y[t][:].indirect(l2[:]))
-            nc.scalar.activation(sa[:, t, :], pa[:, t, :], ACT.Square, scale=2.0)
-            nc.scalar.activation(sq[:, t, :], pb[:, t, :], ACT.Square)
-
-        dt = [sb.tile([P, S], F32, name=f"dt{t}") for t in range(PACK)]
         ra = []
         for half in range(2):
-            ts = slice(2 * half, 2 * half + 2)
-            for t in range(2 * half, 2 * half + 2):
-                nc.vector.tensor_tensor(dt[t][:].indirect(l2[:]), pb[:, t, :], pa[:, t, :], ALU.add)
-            nc.vector.tensor_tensor(ssum[:, ts, :], sa[:, ts, :], sq[:, ts, :], ALU.add)
-            root = sb.tile([P, 2, W], F32, name=f"ra{half}", tag=f"ra{half}", align_bytes=64)
-            nc.scalar.activation(root[:], ssum[:, ts, :], ACT.Sqrt, bias=0.25)
-            ra.append(root)
+            sa = sb.tile([P, 2, W], F32, name=f"sa{half}", tag=f"sa{half}")
+            sq = sb.tile([P, 2, W], F32, name=f"sq{half}", tag=f"sq{half}")
+            for u in range(2):
+                t = 2 * half + u
+                nc.vector.tensor_scalar(pa[:, t, :], y[t][:].indirect(l1[:]), -0.5, 0.0, ALU.mult, ALU.add)
+                nc.vector.tensor_copy(pb[:, t, :], y[t][:].indirect(l2[:]))
+                nc.scalar.activation(sa[:, u, :], pa[:, t, :], ACT.Square, scale=2.0)
+                nc.scalar.activation(sq[:, u, :], pb[:, t, :], ACT.Square)
+            total = bank(5 + half)
+            for u in range(PACK):
+                cols = slice((u % 2) * P, (u % 2 + 1) * P)
+                turn(total[:, u, :], sa[:, u // 2, cols], True, False)
+                turn(total[:, u, :], sq[:, u // 2, cols], False, True)
+            turned = sb.tile([P, PACK, P], F32, name=f"turned{half}", tag=f"turned{half}")
+            nc.scalar.activation(turned[:], total[:], ACT.Sqrt, bias=0.25)
+            back = bank((7, 4)[half])
+            for u in range(PACK):
+                turn(back[:, u, :], turned[:, u, :], True, True)
+            for u in range(2):
+                t = 2 * half + u
+                root = sb.tile([P, 2, P], F32, name=f"ra{t}", tag=f"ra{t}")
+                nc.scalar.copy(root[:], back[:, 2 * u : 2 * u + 2, :])
+                ra.append(root)
 
-        zp = sb.tile([P, PACK, S], BF16, name="zp")
+        dt = [sb.tile([P, S], F32, name=f"dt{t}", tag=tag) for t, tag in enumerate(("sa0", "sq0", "turned0", "sa1"))]
         for t in range(PACK):
-            nc.vector.tensor_copy(dt[t][:].indirect(l1[:]), ra[t // 2][:, t % 2, :])
+            nc.vector.tensor_tensor(dt[t][:].indirect(l2[:]), pb[:, t, :], pa[:, t, :], ALU.add)
+
+        zp = sb.tile([P, PACK, S], BF16, name="zp", tag="zp")
+        for t in range(PACK):
+            nc.vector.tensor_copy(dt[t][:].indirect(l1[:]), ra[t][:].rearrange("p a b -> p (a b)"))
             nc.scalar.activation(zp[:, t, :], dt[t][:], ACT.Copy, scale=gain[:, t : t + 1])
-        zq = sb.tile([P, PACK * S], BF16, name="zq", tag="zq", align_bytes=64)
+        zq = sb.tile([P, PACK * S], BF16, name="zq", align_bytes=64)
         interleave(nc.scalar.copy, zq[:], zp[:])
 
-        y5 = sb.tile([P, PACK, S], F32, name="y5", tag="ra1", align_bytes=64)
-        for t in range(PACK):
-            nc.vector.tensor_copy(y5[:, t, :], y[t][:].indirect(l5[:]))
+        def fetch_y(dst, lst, banks):
+            for t in range(PACK):
+                for c0 in (0, S // 2):
+                    lc = slice(c0 // PER_COL, (c0 + S // 2) // PER_COL)
+                    nc.vector.tensor_copy(dst[:, t, c0 : c0 + S // 2], y[t][:].indirect(lst[:, lc]))
+                for b in range(BLOCKS - 1):
+                    turn(banks[b][:, t, :], dst[:, t, b * P : (b + 1) * P], t == 0, False)
+
+        left_t = [bank(2 * b) for b in range(BLOCKS - 1)]
+        y5 = sb.tile([P, PACK, S], F32, name="y5", tag="ra2")
+        fetch_y(y5, l5, left_t)
 
         zw = sb.tile([P, S], U32, name="zw", align_bytes=64)
         zs = sb.tile([P, S], U8, name="zs", align_bytes=64)
         nc.vector.quantize_mx(out=zw[:].bitcast(FP8X4), scales=zs[:], in_=zq[:])
         h = [sb.tile([P, S], F32, name=f"h{t}") for t in range(PACK)]
         for t in range(PACK):
-            product(w2w, w2s, t, zw, zs, 0, S, h[t], f"bank{t}")
+            product(w2w, w2s, t, zw, zs, 0, S, h[t], f"bank{6 + t % 2}")
 
-        y6 = sb.tile([P, PACK, S], F32, name="y6", tag="zq", align_bytes=64)
-        for t in range(PACK):
-            nc.vector.tensor_copy(y6[:, t, :], y[t][:].indirect(l6[:]))
+        right_t = [bank(2 * b + 1) for b in range(BLOCKS - 1)]
+        y6 = sb.tile([P, PACK, S], F32, name="y6", tag="zp")
+        fetch_y(y6, l6, right_t)
 
         ow = sb.tile([P, S], I32, name="ow", align_bytes=64)
         osc = sb.tile([P, S], U8, name="osc", align_bytes=64)
         out_rows = out_0.rearrange("(p t) j -> p t j", t=PACK)
         out_words = out_1[0].rearrange("p c r -> p (c r)").bitcast(I32)
-        for c0, c1 in PIECES:
-            w = c1 - c0
-            lc = slice(c0 // PER_COL, c1 // PER_COL)
-            left = sb.tile([P, PACK, w], F32, name=f"left{c0}")
-            right = sb.tile([P, PACK, w], F32, name=f"right{c0}")
+
+        def fetch_h(t, b0, b1, got):
+            lc = slice(b0 * P // PER_COL, b1 * P // PER_COL)
+            nc.vector.tensor_copy(got[:, 0, :], h[t][:].indirect(l4[:, lc]))
+            nc.vector.tensor_copy(got[:, 1, :], h[t][:].indirect(l3[:, lc]))
+            for side, banks in enumerate((right_t, left_t)):
+                for b in range(b0, b1):
+                    turn(banks[b][:, t, :], got[:, side, (b - b0) * P : (b - b0 + 1) * P], False, t == PACK - 1)
+
+        def hand_out(b, rq):
+            cols = slice(b * P, (b + 1) * P)
+            nc.vector.quantize_mx(out=ow[:, cols].bitcast(FP8X4), scales=osc[:, cols], in_=rq[:])
+            nc.sync.dma_start(out_words[:, cols], ow[:, cols])
+
+        def finish_turned(b):
+            right = sb.tile([P, PACK, P], F32, name=f"right{b}", tag=f"right{b}")
+            nc.scalar.copy(right[:], right_t[b][:])
+            larger = sb.tile([P, PACK, P], F32, name=f"larger{b}")
+            nc.vector.tensor_tensor(larger[:], right[:], left_t[b][:], ALU.max)
+            back = bank(6 + b % 2)
             for t in range(PACK):
-                nc.vector.tensor_tensor(left[:, t, :], h[t][:].indirect(l3[:, lc]), y5[:, t, c0:c1], ALU.add)
-                nc.vector.tensor_tensor(right[:, t, :], h[t][:].indirect(l4[:, lc]), y6[:, t, c0:c1], ALU.add)
-            res = sb.tile([P, PACK, w], F32, name=f"res{c0}")
-            nc.vector.tensor_tensor(res[:], left[:], right[:], ALU.max)
-            nc.sync.dma_start(out_rows[:, :, c0:c1], res[:])
-            rq = sb.tile([P, PACK * w], BF16, name=f"rq{c0}", align_bytes=64)
-            interleave(nc.scalar.copy, rq[:], res[:])
-            nc.vector.quantize_mx(out=ow[:, c0:c1].bitcast(FP8X4), scales=osc[:, c0:c1], in_=rq[:])
-            nc.sync.dma_start(out_words[:, c0:c1], ow[:, c0:c1])
+                turn(back[:, t, :], larger[:, t, :], True, True)
+            rq = sb.tile([P, PACK * P], BF16, name=f"rq{b}", align_bytes=64)
+            nc.scalar.copy(rq[:].rearrange("p (j t) -> p j t", t=PACK), back[:].rearrange("p t j -> p j t"))
+            res = sb.tile([P, PACK, P], F32, name=f"res{b}")
+            nc.scalar.copy(res[:], back[:])
+            nc.sync.dma_start(out_rows[:, :, b * P : (b + 1) * P], res[:])
+            hand_out(b, rq)
+
+        last = BLOCKS - 1
+        last_cols = slice(last * P, S)
+        last_lc = slice(last * P // PER_COL, S // PER_COL)
+        last_rq = sb.tile([P, PACK * P], BF16, name="last_rq", align_bytes=64)
+        last_pairs = last_rq[:].rearrange("p (j a u) -> p a j u", a=2, u=2)
+
+        def fetch_last(t, left, right):
+            nc.vector.tensor_tensor(left, h[t][:].indirect(l3[:, last_lc]), y5[:, t, last_cols], ALU.add)
+            nc.vector.tensor_tensor(right, h[t][:].indirect(l4[:, last_lc]), y6[:, t, last_cols], ALU.add)
+
+        for t in range(PACK):
+            got = sb.tile([P, 2, 2 * P], F32, name=f"got{t}", tag=f"got{t}")
+            fetch_h(t, 0, 2, got)
+        finish_turned(0)
+        finish_turned(1)
+        got_third = sb.tile([P, PACK, 2, P], F32, name="got_third", tag="got2")
+        for t in range(PACK):
+            fetch_h(t, 2, 3, got_third[:, t])
+        finish_turned(2)
+        sums_first = sb.tile([P, 2, P], F32, name="sums_first", tag="right0")
+        sums_rest = sb.tile([P, 2, PACK - 1, P], F32, name="sums_rest", tag="right2")
+        res_low = sb.tile([P, 2, P], F32, name="res_low")
+        res_high = sb.tile([P, 2, P], F32, name="res_high")
+        fetch_last(0, sums_first[:, 0], sums_first[:, 1])
+        nc.vector.tensor_tensor(res_low[:, 0], sums_first[:, 0], sums_first[:, 1], ALU.max)
+        fetch_last(1, sums_rest[:, 0, 0], sums_rest[:, 1, 0])
+        nc.vector.tensor_tensor(res_low[:, 1], sums_rest[:, 0, 0], sums_rest[:, 1, 0], ALU.max)
+        nc.scalar.copy(last_pairs[:, 0], res_low[:].rearrange("p u j -> p j u"))
+        nc.sync.dma_start(out_rows[:, 0:2, last_cols], res_low[:])
+        for t in (2, 3):
+            fetch_last(t, sums_rest[:, 0, t - 1], sums_rest[:, 1, t - 1])
+        left, right = sums_rest[:, 0, 1:], sums_rest[:, 1, 1:]
+        nc.vector.tensor_tensor(last_pairs[:, 1], left.rearrange("p u j -> p j u"), right.rearrange("p u j -> p j u"), ALU.max)
+        nc.vector.tensor_tensor(res_high[:], left, right, ALU.max)
+        nc.sync.dma_start(out_rows[:, 2:4, last_cols], res_high[:])
+        hand_out(last, last_rq)
         for q in range(QUADS):
             queue = nc.scalar if q % 2 else nc.sync
             queue.dma_start(out_2[0, 4 * q : 4 * q + 4, :].bitcast(I32), osc[32 * q : 32 * q + 4, :].bitcast(I32))

@@ -54,13 +54,11 @@ def tile_picked_skippathbpolar_none_po_kernel(
         def bank(index):
             return psum.tile([P, PACK, P], F32, name=f"bank{index}", tag=f"bank{index}")
 
-        def deal(raw, name, b):
-            dealt = sb.tile([P, PACK, P * b], U8, name=name, align_bytes=64)
+        def deal(dealt, raw, b, ts):
             nc.vector.tensor_copy(
-                dealt[:].rearrange("p t (c i b) -> p c t i b", i=16 // b, b=b),
-                raw[:].rearrange("p (c i t b) -> p c t i b", i=16 // b, t=PACK, b=b),
+                dealt[:].rearrange("p t (c i b) -> p c t i b", i=16 // b, b=b)[:, :, ts],
+                raw[:].rearrange("p (c i t b) -> p c t i b", i=16 // b, t=PACK, b=b)[:, :, ts],
             )
-            return dealt
 
         def interleave(engine_copy, dst, src):
             engine_copy(
@@ -71,9 +69,13 @@ def tile_picked_skippathbpolar_none_po_kernel(
         xs = scale_tile(T, "xs")
         w1s_raw = scale_tile(H, "w1s_raw")
         w2s_raw = scale_tile(N, "w2s_raw")
-        y = [sb.tile([P, S], F32, name=f"y{t}") for t in range(PACK)]
+        y = [sb.tile([P, 2 * S], F32, name=f"y{t}") for t in range(PACK)]
+        for t in range(PACK):
+            nc.vector.memset(y[t][:, S:], 0.0)
         ident = sb.tile([P, P], F32, name="ident")
         make_identity(nc, ident[:])
+        warm = sb.tile([P, 1], F32, name="warm")
+        nc.scalar.activation(warm[:], ident[:, 0:1], ACT.Sqrt, bias=0.25)
 
         w1w_raw = sb.tile([P, 2 * H], U8, name="w1w_raw")
         nc.sync.dma_start(w1w_raw[:].bitcast(I32), w1_words[0].bitcast(I32))
@@ -82,10 +84,10 @@ def tile_picked_skippathbpolar_none_po_kernel(
         xw = sb.tile([P, T], I32, name="xw")
         nc.sync.dma_start(xw[:], x_words[0].rearrange("p c r -> p (c r)").bitcast(I32))
         load_scale_rows(w1s_raw, w1_scales, (nc.sync,) * QUADS)
-        w2w_raw = sb.tile([P, 2 * N], U8, name="w2w_raw")
-        nc.sync.dma_start(w2w_raw[:].bitcast(I32), w2_words[0].bitcast(I32))
         l1 = list_tile(n1, "l1")
         l2 = list_tile(n2, "l2")
+        w2w_raw = sb.tile([P, 2 * N], U8, name="w2w_raw", align_bytes=64)
+        nc.sync.dma_start(w2w_raw[:].bitcast(I32), w2_words[0].bitcast(I32))
         load_scale_rows(w2s_raw, w2_scales, (nc.sync,) * QUADS)
         gain = sb.tile([P, PACK], F32, name="gain")
         nc.sync.dma_start(gain[:], gn.rearrange("(p t) o -> p (t o)", t=PACK))
@@ -94,16 +96,21 @@ def tile_picked_skippathbpolar_none_po_kernel(
         l3 = list_tile(n3, "l3")
         l4 = list_tile(n4, "l4")
 
-        w1w = deal(w1w_raw, "w1w", 2)
+        w1w = sb.tile([P, PACK, 2 * P], U8, name="w1w", align_bytes=64)
+        w1s = sb.tile([P, PACK, P], U8, name="w1s", align_bytes=64)
+        deal(w1w, w1w_raw, 2, slice(0, 1))
         gs = sb.tile([P, S], U8, name="gs", align_bytes=64)
         nc.vector.tensor_copy(gs[:], xs[:].indirect(l_offs[:]))
-        w1s = deal(w1s_raw, "w1s", 1)
+        deal(w1w, w1w_raw, 2, slice(1, PACK))
+        deal(w1s, w1s_raw, 1, slice(0, 1))
         gw = sb.tile([P, S], U32, name="gw", align_bytes=64)
         for c0 in (0, S // 2):
             nc.vector.tensor_copy(
                 gw[:, c0 : c0 + S // 2],
                 xw[:].bitcast(U32).indirect(l_offs[:, c0 // PER_COL : (c0 + S // 2) // PER_COL]),
             )
+
+        deal(w1s, w1s_raw, 1, slice(1, PACK))
 
         def product(ww, ws, t, codes, scales, c0, c1, dst, tag):
             acc = psum.tile([P, c1 - c0], F32, name=tag, tag=tag)
@@ -118,8 +125,6 @@ def tile_picked_skippathbpolar_none_po_kernel(
         for t in range(1, PACK):
             product(w1w, w1s, t, gw, gs, 0, S, y[t], f"bank{t}")
 
-        w2w = deal(w2w_raw, "w2w", 2)
-        w2s = deal(w2s_raw, "w2s", 1)
 
         pa = sb.tile([P, PACK, W], F32, name="pa")
         pb = sb.tile([P, PACK, W], F32, name="pb")
@@ -153,34 +158,51 @@ def tile_picked_skippathbpolar_none_po_kernel(
         for t in range(PACK):
             nc.vector.tensor_tensor(dt[t][:].indirect(l2[:]), pb[:, t, :], pa[:, t, :], ALU.add)
 
-        zp = sb.tile([P, PACK, S], BF16, name="zp", tag="zp")
+        zp = [sb.tile([P, PACK, S // 2], BF16, name=f"zp{half}", tag=f"zp{half}") for half in range(2)]
         for t in range(PACK):
             nc.vector.tensor_copy(dt[t][:].indirect(l1[:]), ra[t][:].rearrange("p a b -> p (a b)"))
-            nc.scalar.activation(zp[:, t, :], dt[t][:], ACT.Copy, scale=gain[:, t : t + 1])
-        zq = sb.tile([P, PACK * S], BF16, name="zq", align_bytes=64)
-        interleave(nc.scalar.copy, zq[:], zp[:])
-
-        def fetch_y(dst, lst, banks):
-            for t in range(PACK):
-                for c0 in (0, S // 2):
-                    lc = slice(c0 // PER_COL, (c0 + S // 2) // PER_COL)
-                    nc.vector.tensor_copy(dst[:, t, c0 : c0 + S // 2], y[t][:].indirect(lst[:, lc]))
-                for b in range(BLOCKS - 1):
-                    turn(banks[b][:, t, :], dst[:, t, b * P : (b + 1) * P], t == 0, False)
-
-        left_t = [bank(2 * b) for b in range(BLOCKS - 1)]
-        y5 = sb.tile([P, PACK, S], F32, name="y5", tag="ra2")
-        fetch_y(y5, l5, left_t)
+            for half in range(2):
+                cols = slice(half * S // 2, (half + 1) * S // 2)
+                nc.scalar.activation(zp[half][:, t, :], dt[t][:, cols], ACT.Copy, scale=gain[:, t : t + 1])
 
         zw = sb.tile([P, S], U32, name="zw", align_bytes=64)
         zs = sb.tile([P, S], U8, name="zs", align_bytes=64)
-        nc.vector.quantize_mx(out=zw[:].bitcast(FP8X4), scales=zs[:], in_=zq[:])
+        h_turned = []
+        for half in range(2):
+            cols = slice(half * S // 2, (half + 1) * S // 2)
+            zq = sb.tile([P, PACK * S // 2], BF16, name=f"zq{half}", align_bytes=64)
+            interleave(nc.scalar.copy, zq[:], zp[half][:])
+            nc.vector.quantize_mx(out=zw[:, cols].bitcast(FP8X4), scales=zs[:, cols], in_=zq[:])
+            for b in (2 * half, 2 * half + 1):
+                acc = psum.tile([P, N], F32, name=f"bank{6 + b % 2}", tag=f"bank{6 + b % 2}")
+                nc.tensor.matmul_mx(
+                    out=acc[:], lhsT=zw[:, b * P : (b + 1) * P].bitcast(FP8X4), lhsT_scale=zs[:, b * P : (b + 1) * P],
+                    rhs=w2w_raw[:].bitcast(FP4X4), rhs_scale=w2s_raw[:], start=True, stop=True,
+                )
+                rows = sb.tile([P, PACK, P], F32, name=f"h_turned{b}")
+                nc.scalar.copy(rows[:], acc[:].rearrange("j (p t) -> j t p", t=PACK))
+                h_turned.append(rows)
         h = [sb.tile([P, S], F32, name=f"h{t}") for t in range(PACK)]
         for t in range(PACK):
-            product(w2w, w2s, t, zw, zs, 0, S, h[t], f"bank{6 + t % 2}")
+            back = bank(6 + t % 2)
+            for b in range(BLOCKS):
+                turn(back[:, b, :], h_turned[b][:, t, :], True, True)
+            nc.scalar.copy(h[t][:], back[:].rearrange("p b j -> p (b j)"))
 
+        def fetch_y(dst, lst, banks):
+            for t in range(PACK):
+                nc.vector.tensor_copy(dst[t], y[t][:].indirect(lst[:]))
+                for b in range(BLOCKS - 1):
+                    turn(banks[b][:, t, :], dst[t][:, b * P : (b + 1) * P], t == 0, False)
+
+        first = sb.tile([P, 2, S], F32, name="y_first", tag="ra2")
+        second = sb.tile([P, S], F32, name="y_second", tag="zp0")
+        rest = sb.tile([P, PACK + 1, S], F32, name="y_rest", tag="zp1")
+        y5 = [first[:, 0], first[:, 1], second[:], rest[:, PACK]]
+        y6 = [rest[:, t] for t in range(PACK)]
+        left_t = [bank(2 * b) for b in range(BLOCKS - 1)]
         right_t = [bank(2 * b + 1) for b in range(BLOCKS - 1)]
-        y6 = sb.tile([P, PACK, S], F32, name="y6", tag="zp")
+        fetch_y(y5, l5, left_t)
         fetch_y(y6, l6, right_t)
 
         ow = sb.tile([P, S], I32, name="ow", align_bytes=64)
@@ -196,12 +218,11 @@ def tile_picked_skippathbpolar_none_po_kernel(
                 for b in range(b0, b1):
                     turn(banks[b][:, t, :], got[:, side, (b - b0) * P : (b - b0 + 1) * P], False, t == PACK - 1)
 
-        def hand_out(b, rq):
-            cols = slice(b * P, (b + 1) * P)
-            nc.vector.quantize_mx(out=ow[:, cols].bitcast(FP8X4), scales=osc[:, cols], in_=rq[:])
-            nc.sync.dma_start(out_words[:, cols], ow[:, cols])
+        def quantize_out(b0, b1, rq):
+            cols = slice(b0 * P, b1 * P)
+            nc.vector.quantize_mx(out=ow[:, cols].bitcast(FP8X4), scales=osc[:, cols], in_=rq)
 
-        def finish_turned(b):
+        def finish_turned(b, rq):
             right = sb.tile([P, PACK, P], F32, name=f"right{b}", tag=f"right{b}")
             nc.scalar.copy(right[:], right_t[b][:])
             larger = sb.tile([P, PACK, P], F32, name=f"larger{b}")
@@ -209,12 +230,10 @@ def tile_picked_skippathbpolar_none_po_kernel(
             back = bank(6 + b % 2)
             for t in range(PACK):
                 turn(back[:, t, :], larger[:, t, :], True, True)
-            rq = sb.tile([P, PACK * P], BF16, name=f"rq{b}", align_bytes=64)
-            nc.scalar.copy(rq[:].rearrange("p (j t) -> p j t", t=PACK), back[:].rearrange("p t j -> p j t"))
+            nc.scalar.copy(rq.rearrange("p (j t) -> p j t", t=PACK), back[:].rearrange("p t j -> p j t"))
             res = sb.tile([P, PACK, P], F32, name=f"res{b}")
             nc.scalar.copy(res[:], back[:])
             nc.sync.dma_start(out_rows[:, :, b * P : (b + 1) * P], res[:])
-            hand_out(b, rq)
 
         last = BLOCKS - 1
         last_cols = slice(last * P, S)
@@ -223,35 +242,40 @@ def tile_picked_skippathbpolar_none_po_kernel(
         last_pairs = last_rq[:].rearrange("p (j a u) -> p a j u", a=2, u=2)
 
         def fetch_last(t, left, right):
-            nc.vector.tensor_tensor(left, h[t][:].indirect(l3[:, last_lc]), y5[:, t, last_cols], ALU.add)
-            nc.vector.tensor_tensor(right, h[t][:].indirect(l4[:, last_lc]), y6[:, t, last_cols], ALU.add)
+            nc.vector.tensor_tensor(left, h[t][:].indirect(l3[:, last_lc]), y5[t][:, last_cols], ALU.add)
+            nc.vector.tensor_tensor(right, h[t][:].indirect(l4[:, last_lc]), y6[t][:, last_cols], ALU.add)
 
         for t in range(PACK):
             got = sb.tile([P, 2, 2 * P], F32, name=f"got{t}", tag=f"got{t}")
             fetch_h(t, 0, 2, got)
-        finish_turned(0)
-        finish_turned(1)
+        rq_front = sb.tile([P, 2 * PACK * P], BF16, name="rq_front", align_bytes=64)
+        finish_turned(0, rq_front[:, : PACK * P])
+        finish_turned(1, rq_front[:, PACK * P :])
+        quantize_out(0, 2, rq_front[:])
+        nc.sync.dma_start(out_words[:, : 2 * P], ow[:, : 2 * P])
         got_third = sb.tile([P, PACK, 2, P], F32, name="got_third", tag="got2")
         for t in range(PACK):
             fetch_h(t, 2, 3, got_third[:, t])
-        finish_turned(2)
-        sums_first = sb.tile([P, 2, P], F32, name="sums_first", tag="right0")
-        sums_rest = sb.tile([P, 2, PACK - 1, P], F32, name="sums_rest", tag="right2")
+        rq_third = sb.tile([P, PACK * P], BF16, name="rq_third", align_bytes=64)
+        finish_turned(2, rq_third[:])
+        quantize_out(2, 3, rq_third[:])
+        sums_low = sb.tile([P, 2, 2, P], F32, name="sums_low", tag="right0")
+        sums_high = sb.tile([P, 2, 2, P], F32, name="sums_high", tag="right2")
         res_low = sb.tile([P, 2, P], F32, name="res_low")
         res_high = sb.tile([P, 2, P], F32, name="res_high")
-        fetch_last(0, sums_first[:, 0], sums_first[:, 1])
-        nc.vector.tensor_tensor(res_low[:, 0], sums_first[:, 0], sums_first[:, 1], ALU.max)
-        fetch_last(1, sums_rest[:, 0, 0], sums_rest[:, 1, 0])
-        nc.vector.tensor_tensor(res_low[:, 1], sums_rest[:, 0, 0], sums_rest[:, 1, 0], ALU.max)
+        for t in (0, 1):
+            fetch_last(t, sums_low[:, 0, t], sums_low[:, 1, t])
+        nc.vector.tensor_tensor(res_low[:], sums_low[:, 0], sums_low[:, 1], ALU.max)
         nc.scalar.copy(last_pairs[:, 0], res_low[:].rearrange("p u j -> p j u"))
         nc.sync.dma_start(out_rows[:, 0:2, last_cols], res_low[:])
         for t in (2, 3):
-            fetch_last(t, sums_rest[:, 0, t - 1], sums_rest[:, 1, t - 1])
-        left, right = sums_rest[:, 0, 1:], sums_rest[:, 1, 1:]
+            fetch_last(t, sums_high[:, 0, t - 2], sums_high[:, 1, t - 2])
+        left, right = sums_high[:, 0], sums_high[:, 1]
         nc.vector.tensor_tensor(last_pairs[:, 1], left.rearrange("p u j -> p j u"), right.rearrange("p u j -> p j u"), ALU.max)
         nc.vector.tensor_tensor(res_high[:], left, right, ALU.max)
         nc.sync.dma_start(out_rows[:, 2:4, last_cols], res_high[:])
-        hand_out(last, last_rq)
+        quantize_out(last, BLOCKS, last_rq[:])
+        nc.sync.dma_start(out_words[:, 2 * P :], ow[:, 2 * P :])
         for q in range(QUADS):
             queue = nc.scalar if q % 2 else nc.sync
             queue.dma_start(out_2[0, 4 * q : 4 * q + 4, :].bitcast(I32), osc[32 * q : 32 * q + 4, :].bitcast(I32))

@@ -21,7 +21,12 @@ P = 128
 PACK = 4
 QUADS = 4
 PER_COL = 16
+LINE = 16
 BLOCKS = S // P
+TURNED = PACK - 1
+LAST = PACK - 1
+PIECES = ((0, 256), (256, 384), (384, 512))
+SPANS = (((0, BLOCKS, 0, 3),), ((0, BLOCKS, 1, 4),), ((0, 2, 2, 5), (2, BLOCKS, 7, 6)))
 
 
 def tile_picked_skippathbpolar_none_po_kernel(
@@ -40,7 +45,7 @@ def tile_picked_skippathbpolar_none_po_kernel(
             return tile
 
         def scale_tile(width, name):
-            tile = sb.tile([P, width], U8, name=name, align_bytes=64)
+            tile = sb.tile([P, width], U8, name=name, tag=name, align_bytes=64)
             nc.vector.memset(tile[:].bitcast(I32), 0)
             return tile
 
@@ -56,8 +61,8 @@ def tile_picked_skippathbpolar_none_po_kernel(
 
         def deal(dealt, raw, b, ts):
             nc.vector.tensor_copy(
-                dealt[:].rearrange("p t (c i b) -> p c t i b", i=16 // b, b=b)[:, :, ts],
-                raw[:].rearrange("p (c i t b) -> p c t i b", i=16 // b, t=PACK, b=b)[:, :, ts],
+                dealt[:].rearrange("p t (c i b) -> p c t i b", i=LINE // b, b=b)[:, :, ts],
+                raw[:].rearrange("p (c i t b) -> p c t i b", i=LINE // b, t=PACK, b=b)[:, :, ts],
             )
 
         def interleave(engine_copy, dst, src):
@@ -77,17 +82,20 @@ def tile_picked_skippathbpolar_none_po_kernel(
         warm = sb.tile([P, 1], F32, name="warm")
         nc.scalar.activation(warm[:], ident[:, 0:1], ACT.Sqrt, bias=0.25)
 
+        h = [sb.tile([P, 2 * S], F32, name=f"h{t}", tag=f"h{t}") for t in range(TURNED)]
+        h.append(sb.tile([P, S], F32, name="h_last"))
+
         w1w_raw = sb.tile([P, 2 * H], U8, name="w1w_raw")
         nc.sync.dma_start(w1w_raw[:].bitcast(I32), w1_words[0].bitcast(I32))
         l_offs = list_tile(offs, "l_offs")
         load_scale_rows(xs, x_scales, (nc.sync, nc.sync, nc.scalar, nc.scalar))
-        xw = sb.tile([P, T], I32, name="xw")
+        xw = sb.tile([P, T], I32, name="xw", tag="xw", align_bytes=64)
         nc.sync.dma_start(xw[:], x_words[0].rearrange("p c r -> p (c r)").bitcast(I32))
         load_scale_rows(w1s_raw, w1_scales, (nc.sync,) * QUADS)
+        w2w_raw = sb.tile([P, 2 * N], U8, name="w2w_raw")
+        nc.sync.dma_start(w2w_raw[:].bitcast(I32), w2_words[0].bitcast(I32))
         l1 = list_tile(n1, "l1")
         l2 = list_tile(n2, "l2")
-        w2w_raw = sb.tile([P, 2 * N], U8, name="w2w_raw", align_bytes=64)
-        nc.sync.dma_start(w2w_raw[:].bitcast(I32), w2_words[0].bitcast(I32))
         load_scale_rows(w2s_raw, w2_scales, (nc.sync,) * QUADS)
         gain = sb.tile([P, PACK], F32, name="gain")
         nc.sync.dma_start(gain[:], gn.rearrange("(p t) o -> p (t o)", t=PACK))
@@ -96,20 +104,17 @@ def tile_picked_skippathbpolar_none_po_kernel(
         l3 = list_tile(n3, "l3")
         l4 = list_tile(n4, "l4")
 
+        for t in range(TURNED):
+            nc.scalar.copy(h[t][:, S:], y[0][:, S:])
+
         w1w = sb.tile([P, PACK, 2 * P], U8, name="w1w", align_bytes=64)
-        w1s = sb.tile([P, PACK, P], U8, name="w1s", align_bytes=64)
-        deal(w1w, w1w_raw, 2, slice(0, 1))
+        deal(w1w, w1w_raw, 2, slice(0, PACK))
         gs = sb.tile([P, S], U8, name="gs", align_bytes=64)
         nc.vector.tensor_copy(gs[:], xs[:].indirect(l_offs[:]))
-        deal(w1w, w1w_raw, 2, slice(1, PACK))
-        deal(w1s, w1s_raw, 1, slice(0, 1))
         gw = sb.tile([P, S], U32, name="gw", align_bytes=64)
-        for c0 in (0, S // 2):
-            nc.vector.tensor_copy(
-                gw[:, c0 : c0 + S // 2],
-                xw[:].bitcast(U32).indirect(l_offs[:, c0 // PER_COL : (c0 + S // 2) // PER_COL]),
-            )
-
+        nc.vector.tensor_copy(gw[:], xw[:].bitcast(U32).indirect(l_offs[:]))
+        w1s = sb.tile([P, PACK, P], U8, name="w1s", tag="xw", align_bytes=64)
+        deal(w1s, w1s_raw, 1, slice(0, 1))
         deal(w1s, w1s_raw, 1, slice(1, PACK))
 
         def product(ww, ws, t, codes, scales, c0, c1, dst, tag):
@@ -125,157 +130,130 @@ def tile_picked_skippathbpolar_none_po_kernel(
         for t in range(1, PACK):
             product(w1w, w1s, t, gw, gs, 0, S, y[t], f"bank{t}")
 
+        w2w = sb.tile([P, PACK, 2 * P], U8, name="w2w", tag="w1s_raw", align_bytes=64)
+        deal(w2w, w2w_raw, 2, slice(0, PACK))
 
-        pa = sb.tile([P, PACK, W], F32, name="pa")
+        pa_half = sb.tile([P, PACK, W], F32, name="pa_half")
         pb = sb.tile([P, PACK, W], F32, name="pb")
         ra = []
-        for half in range(2):
-            sa = sb.tile([P, 2, W], F32, name=f"sa{half}", tag=f"sa{half}")
-            sq = sb.tile([P, 2, W], F32, name=f"sq{half}", tag=f"sq{half}")
+        for pair in range(2):
+            pa_sq = sb.tile([P, 2, W], F32, name=f"pa_sq{pair}", tag=f"pa_sq{pair}")
+            pb_sq = sb.tile([P, 2, W], F32, name=f"pb_sq{pair}", tag=f"pb_sq{pair}")
             for u in range(2):
-                t = 2 * half + u
-                nc.vector.tensor_scalar(pa[:, t, :], y[t][:].indirect(l1[:]), -0.5, 0.0, ALU.mult, ALU.add)
+                t = 2 * pair + u
+                nc.vector.tensor_scalar(pa_half[:, t, :], y[t][:].indirect(l1[:]), -0.5, 0.0, ALU.mult, ALU.add)
                 nc.vector.tensor_copy(pb[:, t, :], y[t][:].indirect(l2[:]))
-                nc.scalar.activation(sa[:, u, :], pa[:, t, :], ACT.Square, scale=2.0)
-                nc.scalar.activation(sq[:, u, :], pb[:, t, :], ACT.Square)
-            total = bank(5 + half)
-            for u in range(PACK):
-                cols = slice((u % 2) * P, (u % 2 + 1) * P)
-                turn(total[:, u, :], sa[:, u // 2, cols], True, False)
-                turn(total[:, u, :], sq[:, u // 2, cols], False, True)
-            turned = sb.tile([P, PACK, P], F32, name=f"turned{half}", tag=f"turned{half}")
-            nc.scalar.activation(turned[:], total[:], ACT.Sqrt, bias=0.25)
-            back = bank((7, 4)[half])
-            for u in range(PACK):
-                turn(back[:, u, :], turned[:, u, :], True, True)
+                nc.scalar.activation(pa_sq[:, u, :], pa_half[:, t, :], ACT.Square, scale=2.0)
+                nc.scalar.activation(pb_sq[:, u, :], pb[:, t, :], ACT.Square)
+            squares = bank(5 + pair)
+            for v in range(PACK):
+                cols = slice((v % 2) * P, (v % 2 + 1) * P)
+                turn(squares[:, v, :], pa_sq[:, v // 2, cols], True, False)
+                turn(squares[:, v, :], pb_sq[:, v // 2, cols], False, True)
+            roots_turned = sb.tile([P, PACK, P], F32, name=f"roots_turned{pair}", tag=f"roots_turned{pair}")
+            nc.scalar.activation(roots_turned[:], squares[:], ACT.Sqrt, bias=0.25)
+            roots = bank((7, 4)[pair])
+            for v in range(PACK):
+                turn(roots[:, v, :], roots_turned[:, v, :], True, True)
             for u in range(2):
-                t = 2 * half + u
-                root = sb.tile([P, 2, P], F32, name=f"ra{t}", tag=f"ra{t}")
-                nc.scalar.copy(root[:], back[:, 2 * u : 2 * u + 2, :])
-                ra.append(root)
+                t = 2 * pair + u
+                ra_t = sb.tile([P, 2, P], F32, name=f"ra{t}", tag=f"ra{t}", align_bytes=64)
+                nc.scalar.copy(ra_t[:], roots[:, 2 * u : 2 * u + 2, :])
+                ra.append(ra_t)
 
-        dt = [sb.tile([P, S], F32, name=f"dt{t}", tag=tag) for t, tag in enumerate(("sa0", "sq0", "turned0", "sa1"))]
+        dt_tags = ("pa_sq0", "pb_sq0", "roots_turned0", "pa_sq1")
+        dt = [sb.tile([P, S], F32, name=f"dt{t}", tag=dt_tags[t]) for t in range(PACK)]
         for t in range(PACK):
-            nc.vector.tensor_tensor(dt[t][:].indirect(l2[:]), pb[:, t, :], pa[:, t, :], ALU.add)
+            nc.vector.tensor_tensor(dt[t][:].indirect(l2[:]), pb[:, t, :], pa_half[:, t, :], ALU.add)
 
-        zp = [sb.tile([P, PACK, S // 2], BF16, name=f"zp{half}", tag=f"zp{half}") for half in range(2)]
+        z_planes = sb.tile([P, PACK, S], BF16, name="z_planes", tag="z_planes")
         for t in range(PACK):
             nc.vector.tensor_copy(dt[t][:].indirect(l1[:]), ra[t][:].rearrange("p a b -> p (a b)"))
-            for half in range(2):
-                cols = slice(half * S // 2, (half + 1) * S // 2)
-                nc.scalar.activation(zp[half][:, t, :], dt[t][:, cols], ACT.Copy, scale=gain[:, t : t + 1])
-
+            nc.scalar.activation(z_planes[:, t, :], dt[t][:], ACT.Copy, scale=gain[:, t : t + 1])
+        w2s = sb.tile([P, PACK, P], U8, name="w2s", tag="ra0", align_bytes=64)
+        deal(w2s, w2s_raw, 1, slice(0, PACK))
+        zq = sb.tile([P, PACK * S], BF16, name="zq", align_bytes=64)
+        interleave(nc.scalar.copy, zq[:], z_planes[:])
         zw = sb.tile([P, S], U32, name="zw", align_bytes=64)
         zs = sb.tile([P, S], U8, name="zs", align_bytes=64)
-        h_turned = []
-        for half in range(2):
-            cols = slice(half * S // 2, (half + 1) * S // 2)
-            zq = sb.tile([P, PACK * S // 2], BF16, name=f"zq{half}", align_bytes=64)
-            interleave(nc.scalar.copy, zq[:], zp[half][:])
-            nc.vector.quantize_mx(out=zw[:, cols].bitcast(FP8X4), scales=zs[:, cols], in_=zq[:])
-            for b in (2 * half, 2 * half + 1):
-                acc = psum.tile([P, N], F32, name=f"bank{6 + b % 2}", tag=f"bank{6 + b % 2}")
-                nc.tensor.matmul_mx(
-                    out=acc[:], lhsT=zw[:, b * P : (b + 1) * P].bitcast(FP8X4), lhsT_scale=zs[:, b * P : (b + 1) * P],
-                    rhs=w2w_raw[:].bitcast(FP4X4), rhs_scale=w2s_raw[:], start=True, stop=True,
-                )
-                rows = sb.tile([P, PACK, P], F32, name=f"h_turned{b}")
-                nc.scalar.copy(rows[:], acc[:].rearrange("j (p t) -> j t p", t=PACK))
-                h_turned.append(rows)
-        h = [sb.tile([P, S], F32, name=f"h{t}") for t in range(PACK)]
+        nc.vector.quantize_mx(out=zw[:].bitcast(FP8X4), scales=zs[:], in_=zq[:])
         for t in range(PACK):
-            back = bank(6 + t % 2)
-            for b in range(BLOCKS):
-                turn(back[:, b, :], h_turned[b][:, t, :], True, True)
-            nc.scalar.copy(h[t][:], back[:].rearrange("p b j -> p (b j)"))
+            product(w2w, w2s, t, zw, zs, 0, S, h[t], f"bank{TURNED + t}")
 
-        def fetch_y(dst, lst, banks):
-            for t in range(PACK):
-                nc.vector.tensor_copy(dst[t], y[t][:].indirect(lst[:]))
-                for b in range(BLOCKS - 1):
-                    turn(banks[b][:, t, :], dst[t][:, b * P : (b + 1) * P], t == 0, False)
+        totals = {(t, b0): bank(sum_bank) for t in range(TURNED) for b0, b1, sum_bank, back_bank in SPANS[t]}
 
-        first = sb.tile([P, 2, S], F32, name="y_first", tag="ra2")
-        second = sb.tile([P, S], F32, name="y_second", tag="zp0")
-        rest = sb.tile([P, PACK + 1, S], F32, name="y_rest", tag="zp1")
-        y5 = [first[:, 0], first[:, 1], second[:], rest[:, PACK]]
-        y6 = [rest[:, t] for t in range(PACK)]
-        left_t = [bank(2 * b) for b in range(BLOCKS - 1)]
-        right_t = [bank(2 * b + 1) for b in range(BLOCKS - 1)]
-        fetch_y(y5, l5, left_t)
-        fetch_y(y6, l6, right_t)
+        def add_turned(t, b0, b1, src, start, stop):
+            for b in range(b0, b1):
+                turn(totals[t, b0][:, b, :], src[:, b * P : (b + 1) * P], start and b == b0, stop and b == b1 - 1)
+
+        y6 = sb.tile([P, TURNED, S], F32, name="y6", tag="ra2", align_bytes=64)
+        diff = sb.tile([P, TURNED, S], F32, name="diff", tag="z_planes")
+        for t in range(TURNED):
+            nc.vector.tensor_copy(y6[:, t], y[t][:].indirect(l6[:]))
+            for b0, b1, sum_bank, back_bank in SPANS[t]:
+                add_turned(t, b0, b1, y6[:, t], True, False)
+        for t in range(TURNED):
+            nc.vector.tensor_tensor(diff[:, t], y[t][:].indirect(l5[:]), y6[:, t], ALU.subtract)
+
+        res = [sb.tile([P, PACK, c1 - c0], F32, name=f"res{c0}") for c0, c1 in PIECES]
+        part = sb.tile([P, TURNED, S], F32, name="part")
+
+        def fetch_part(t):
+            nc.vector.tensor_tensor(part[:, t], h[t][:].indirect(l3[:]), diff[:, t], ALU.add)
+            for b0, b1, sum_bank, back_bank in SPANS[t]:
+                add_turned(t, b0, b1, part[:, t], False, False)
+
+        def fetch_excess(t):
+            nc.vector.tensor_tensor(diff[:, t], h[t][:].indirect(l4[:]), part[:, t], ALU.subtract)
+            over = sb.tile([P, S], F32, name=f"over{t}")
+            for b0, b1, sum_bank, back_bank in SPANS[t]:
+                nc.scalar.activation(over[:, b0 * P : b1 * P], diff[:, t, b0 * P : b1 * P], ACT.Relu)
+                add_turned(t, b0, b1, over[:], False, True)
+
+        backs = {}
+
+        def turn_back(t):
+            larger = sb.tile([P, BLOCKS, P], F32, name=f"larger{t}")
+            for b0, b1, sum_bank, back_bank in SPANS[t]:
+                nc.scalar.copy(larger[:, b0:b1], totals[t, b0][:, b0:b1])
+                back = bank(back_bank)
+                for b in range(b0, b1):
+                    turn(back[:, b, :], larger[:, b, :], True, True)
+                    backs[t, b] = back
+
+        for group in ((0, 1), (2,)):
+            for step in (fetch_part, fetch_excess, turn_back):
+                for t in group:
+                    step(t)
+        for piece, (c0, c1) in zip(res, PIECES):
+            for t in range(TURNED):
+                nc.scalar.copy(piece[:, t, :], backs[t, c0 // P][:].rearrange("p b j -> p (b j)")[:, c0:c1])
 
         ow = sb.tile([P, S], I32, name="ow", align_bytes=64)
         osc = sb.tile([P, S], U8, name="osc", align_bytes=64)
         out_rows = out_0.rearrange("(p t) j -> p t j", t=PACK)
         out_words = out_1[0].rearrange("p c r -> p (c r)").bitcast(I32)
 
-        def fetch_h(t, b0, b1, got):
-            lc = slice(b0 * P // PER_COL, b1 * P // PER_COL)
-            nc.vector.tensor_copy(got[:, 0, :], h[t][:].indirect(l4[:, lc]))
-            nc.vector.tensor_copy(got[:, 1, :], h[t][:].indirect(l3[:, lc]))
-            for side, banks in enumerate((right_t, left_t)):
-                for b in range(b0, b1):
-                    turn(banks[b][:, t, :], got[:, side, (b - b0) * P : (b - b0 + 1) * P], False, t == PACK - 1)
-
-        def quantize_out(b0, b1, rq):
-            cols = slice(b0 * P, b1 * P)
-            nc.vector.quantize_mx(out=ow[:, cols].bitcast(FP8X4), scales=osc[:, cols], in_=rq)
-
-        def finish_turned(b, rq):
-            right = sb.tile([P, PACK, P], F32, name=f"right{b}", tag=f"right{b}")
-            nc.scalar.copy(right[:], right_t[b][:])
-            larger = sb.tile([P, PACK, P], F32, name=f"larger{b}")
-            nc.vector.tensor_tensor(larger[:], right[:], left_t[b][:], ALU.max)
-            back = bank(6 + b % 2)
-            for t in range(PACK):
-                turn(back[:, t, :], larger[:, t, :], True, True)
-            nc.scalar.copy(rq.rearrange("p (j t) -> p j t", t=PACK), back[:].rearrange("p t j -> p j t"))
-            res = sb.tile([P, PACK, P], F32, name=f"res{b}")
-            nc.scalar.copy(res[:], back[:])
-            nc.sync.dma_start(out_rows[:, :, b * P : (b + 1) * P], res[:])
-
-        last = BLOCKS - 1
-        last_cols = slice(last * P, S)
-        last_lc = slice(last * P // PER_COL, S // PER_COL)
-        last_rq = sb.tile([P, PACK * P], BF16, name="last_rq", align_bytes=64)
-        last_pairs = last_rq[:].rearrange("p (j a u) -> p a j u", a=2, u=2)
-
-        def fetch_last(t, left, right):
-            nc.vector.tensor_tensor(left, h[t][:].indirect(l3[:, last_lc]), y5[t][:, last_cols], ALU.add)
-            nc.vector.tensor_tensor(right, h[t][:].indirect(l4[:, last_lc]), y6[t][:, last_cols], ALU.add)
-
-        for t in range(PACK):
-            got = sb.tile([P, 2, 2 * P], F32, name=f"got{t}", tag=f"got{t}")
-            fetch_h(t, 0, 2, got)
-        rq_front = sb.tile([P, 2 * PACK * P], BF16, name="rq_front", align_bytes=64)
-        finish_turned(0, rq_front[:, : PACK * P])
-        finish_turned(1, rq_front[:, PACK * P :])
-        quantize_out(0, 2, rq_front[:])
-        nc.sync.dma_start(out_words[:, : 2 * P], ow[:, : 2 * P])
-        got_third = sb.tile([P, PACK, 2, P], F32, name="got_third", tag="got2")
-        for t in range(PACK):
-            fetch_h(t, 2, 3, got_third[:, t])
-        rq_third = sb.tile([P, PACK * P], BF16, name="rq_third", align_bytes=64)
-        finish_turned(2, rq_third[:])
-        quantize_out(2, 3, rq_third[:])
-        sums_low = sb.tile([P, 2, 2, P], F32, name="sums_low", tag="right0")
-        sums_high = sb.tile([P, 2, 2, P], F32, name="sums_high", tag="right2")
-        res_low = sb.tile([P, 2, P], F32, name="res_low")
-        res_high = sb.tile([P, 2, P], F32, name="res_high")
-        for t in (0, 1):
-            fetch_last(t, sums_low[:, 0, t], sums_low[:, 1, t])
-        nc.vector.tensor_tensor(res_low[:], sums_low[:, 0], sums_low[:, 1], ALU.max)
-        nc.scalar.copy(last_pairs[:, 0], res_low[:].rearrange("p u j -> p j u"))
-        nc.sync.dma_start(out_rows[:, 0:2, last_cols], res_low[:])
-        for t in (2, 3):
-            fetch_last(t, sums_high[:, 0, t - 2], sums_high[:, 1, t - 2])
-        left, right = sums_high[:, 0], sums_high[:, 1]
-        nc.vector.tensor_tensor(last_pairs[:, 1], left.rearrange("p u j -> p j u"), right.rearrange("p u j -> p j u"), ALU.max)
-        nc.vector.tensor_tensor(res_high[:], left, right, ALU.max)
-        nc.sync.dma_start(out_rows[:, 2:4, last_cols], res_high[:])
-        quantize_out(last, BLOCKS, last_rq[:])
-        nc.sync.dma_start(out_words[:, 2 * P :], ow[:, 2 * P :])
+        y_last = sb.tile([P, 2, S], F32, name="y_last", tag=f"h{TURNED - 1}")
+        nc.vector.tensor_copy(y_last[:, 0], y[LAST][:].indirect(l5[:]))
+        nc.vector.tensor_copy(y_last[:, 1], y[LAST][:].indirect(l6[:]))
+        for piece, (c0, c1) in zip(res, PIECES):
+            list_cols = slice(c0 // PER_COL, c1 // PER_COL)
+            sums = sb.tile([P, 2, c1 - c0], F32, name=f"sums{c0}")
+            nc.vector.tensor_tensor(sums[:, 0], h[LAST][:].indirect(l3[:, list_cols]), y_last[:, 0, c0:c1], ALU.add)
+            nc.vector.tensor_tensor(sums[:, 1], h[LAST][:].indirect(l4[:, list_cols]), y_last[:, 1, c0:c1], ALU.add)
+            nc.vector.tensor_tensor(piece[:, LAST], sums[:, 0], sums[:, 1], ALU.max)
+            nc.sync.dma_start(out_rows[:, :, c0:c1], piece[:])
+        for piece, (c0, c1) in zip(res, PIECES):
+            is_last = c1 == S
+            rounded = sb.tile(
+                [P, PACK * (c1 - c0)], BF16, name=f"rounded{c0}", tag=f"rounded{0 if is_last else c0}", align_bytes=64
+            )
+            interleave(nc.vector.tensor_copy if is_last else nc.scalar.copy, rounded[:], piece[:])
+            nc.vector.quantize_mx(out=ow[:, c0:c1].bitcast(FP8X4), scales=osc[:, c0:c1], in_=rounded[:])
+            if c0 > 0:
+                w0 = c0 if is_last else 0
+                nc.sync.dma_start(out_words[:, w0:c1], ow[:, w0:c1])
         for q in range(QUADS):
             queue = nc.scalar if q % 2 else nc.sync
             queue.dma_start(out_2[0, 4 * q : 4 * q + 4, :].bitcast(I32), osc[32 * q : 32 * q + 4, :].bitcast(I32))

from contextlib import ExitStack

import concourse.mybir as mybir
from concourse.masks import make_identity

K, T, S, N, H, W = 512, 2048, 512, 512, 512, 256
FLOPS = 2 * K * H * S + 2 * H * N * S

F32 = mybir.dt.float32
BF16 = mybir.dt.bfloat16
I32 = mybir.dt.int32
U32 = mybir.dt.uint32
U16 = mybir.dt.uint16
U8 = mybir.dt.uint8
FP8X4 = mybir.dt.float8_e4m3fn_x4
FP4X4 = mybir.dt.float4_e2m1fn_x4
ALU = mybir.AluOpType
ACT = mybir.ActivationFunctionType

P = 128
PACK = 4
QUADS = 4
PER_COL = 16
LINE = 16
BLOCKS = S // P
TURNED = PACK - 1
LAST = PACK - 1
PIECES = ((0, 256), (256, 384), (384, 512))
SPANS = (((0, BLOCKS, 0, 3),), ((0, BLOCKS, 1, 4),), ((0, 2, 2, 5), (2, BLOCKS, 7, 6)))


def tile_picked_skippathbpolar_none_po_kernel(
    tc, x_words, x_scales, w1_words, w1_scales, gn, w2_words, w2_scales,
    offs, n1, n2, n3, n4, n5, n6, out_0, out_1, out_2,
):
    nc = tc.nc
    with ExitStack() as ctx:
        lists = ctx.enter_context(tc.tile_pool(name="lists", bufs=1))
        sb = ctx.enter_context(tc.tile_pool(name="sb", bufs=1))
        psum = ctx.enter_context(tc.psum_pool(name="psum", bufs=1))

        def list_tile(src, name):
            tile = lists.tile(list(src.shape), U16, name=name)
            nc.sync.dma_start(tile[:], src)
            return tile

        def scale_tile(width, name):
            tile = sb.tile([P, width], U8, name=name, tag=name, align_bytes=64)
            nc.vector.memset(tile[:].bitcast(I32), 0)
            return tile

        def load_scale_rows(tile, src, queues):
            for q in range(QUADS):
                queues[q].dma_start(tile[32 * q : 32 * q + 4, :].bitcast(I32), src[0, 4 * q : 4 * q + 4, :].bitcast(I32))

        def turn(dst, src, start, stop):
            nc.tensor.matmul(dst, lhsT=src, rhs=ident[:], start=start, stop=stop, is_transpose=True)

        def bank(index):
            return psum.tile([P, PACK, P], F32, name=f"bank{index}", tag=f"bank{index}")

        def deal(dealt, raw, b, ts):
            nc.vector.tensor_copy(
                dealt[:].rearrange("p t (c i b) -> p c t i b", i=LINE // b, b=b)[:, :, ts],
                raw[:].rearrange("p (c i t b) -> p c t i b", i=LINE // b, t=PACK, b=b)[:, :, ts],
            )

        def interleave(engine_copy, dst, src):
            engine_copy(
                dst.rearrange("p (c i t) -> p c t i", i=4, t=PACK),
                src.rearrange("p t (c i) -> p c t i", i=4),
            )

        xs = scale_tile(T, "xs")
        w1s_raw = scale_tile(H, "w1s_raw")
        w2s_raw = scale_tile(N, "w2s_raw")
        y = [sb.tile([P, 2 * S], F32, name=f"y{t}") for t in range(PACK)]
        for t in range(PACK):
            nc.vector.memset(y[t][:, S:], 0.0)
        ident = sb.tile([P, P], F32, name="ident")
        make_identity(nc, ident[:])
        warm = sb.tile([P, 1], F32, name="warm")
        nc.scalar.activation(warm[:], ident[:, 0:1], ACT.Sqrt, bias=0.25)

        h = [sb.tile([P, 2 * S], F32, name=f"h{t}", tag=f"h{t}") for t in range(TURNED)]
        h.append(sb.tile([P, S], F32, name="h_last"))

        w1w_raw = sb.tile([P, 2 * H], U8, name="w1w_raw")
        nc.sync.dma_start(w1w_raw[:].bitcast(I32), w1_words[0].bitcast(I32))
        l_offs = list_tile(offs, "l_offs")
        load_scale_rows(xs, x_scales, (nc.sync, nc.sync, nc.scalar, nc.scalar))
        xw = sb.tile([P, T], I32, name="xw", tag="xw", align_bytes=64)
        nc.sync.dma_start(xw[:], x_words[0].rearrange("p c r -> p (c r)").bitcast(I32))
        load_scale_rows(w1s_raw, w1_scales, (nc.sync,) * QUADS)
        w2w_raw = sb.tile([P, 2 * N], U8, name="w2w_raw")
        nc.sync.dma_start(w2w_raw[:].bitcast(I32), w2_words[0].bitcast(I32))
        l1 = list_tile(n1, "l1")
        l2 = list_tile(n2, "l2")
        load_scale_rows(w2s_raw, w2_scales, (nc.sync,) * QUADS)
        gain = sb.tile([P, PACK], F32, name="gain")
        nc.sync.dma_start(gain[:], gn.rearrange("(p t) o -> p (t o)", t=PACK))
        l5 = list_tile(n5, "l5")
        l6 = list_tile(n6, "l6")
        l3 = list_tile(n3, "l3")
        l4 = list_tile(n4, "l4")

        for t in range(TURNED):
            nc.scalar.copy(h[t][:, S:], y[0][:, S:])

        w1w = sb.tile([P, PACK, 2 * P], U8, name="w1w", align_bytes=64)
        deal(w1w, w1w_raw, 2, slice(0, PACK))
        gs = sb.tile([P, S], U8, name="gs", align_bytes=64)
        nc.vector.tensor_copy(gs[:], xs[:].indirect(l_offs[:]))
        gw = sb.tile([P, S], U32, name="gw", align_bytes=64)
        nc.vector.tensor_copy(gw[:], xw[:].bitcast(U32).indirect(l_offs[:]))
        w1s = sb.tile([P, PACK, P], U8, name="w1s", tag="xw", align_bytes=64)
        deal(w1s, w1s_raw, 1, slice(0, 1))
        deal(w1s, w1s_raw, 1, slice(1, PACK))

        def product(ww, ws, t, codes, scales, c0, c1, dst, tag):
            acc = psum.tile([P, c1 - c0], F32, name=tag, tag=tag)
            nc.tensor.matmul_mx(
                out=acc[:], lhsT=ww[:, t, :].bitcast(FP4X4), lhsT_scale=ws[:, t, :],
                rhs=codes[:, c0:c1].bitcast(FP8X4), rhs_scale=scales[:, c0:c1], start=True, stop=True,
            )
            nc.scalar.copy(dst[:, c0:c1], acc[:])

        product(w1w, w1s, 0, gw, gs, 0, S // 2, y[0], "bank4")
        product(w1w, w1s, 0, gw, gs, S // 2, S, y[0], "bank0")
        for t in range(1, PACK):
            product(w1w, w1s, t, gw, gs, 0, S, y[t], f"bank{t}")

        w2w = sb.tile([P, PACK, 2 * P], U8, name="w2w", tag="w1s_raw", align_bytes=64)
        deal(w2w, w2w_raw, 2, slice(0, PACK))

        pa_half = sb.tile([P, PACK, W], F32, name="pa_half")
        pb = sb.tile([P, PACK, W], F32, name="pb")
        ra = []
        for pair in range(2):
            pa_sq = sb.tile([P, 2, W], F32, name=f"pa_sq{pair}", tag=f"pa_sq{pair}")
            pb_sq = sb.tile([P, 2, W], F32, name=f"pb_sq{pair}", tag=f"pb_sq{pair}")
            for u in range(2):
                t = 2 * pair + u
                nc.vector.tensor_scalar(pa_half[:, t, :], y[t][:].indirect(l1[:]), -0.5, 0.0, ALU.mult, ALU.add)
                nc.vector.tensor_copy(pb[:, t, :], y[t][:].indirect(l2[:]))
                nc.scalar.activation(pa_sq[:, u, :], pa_half[:, t, :], ACT.Square, scale=2.0)
                nc.scalar.activation(pb_sq[:, u, :], pb[:, t, :], ACT.Square)
            squares = bank(5 + pair)
            for v in range(PACK):
                cols = slice((v % 2) * P, (v % 2 + 1) * P)
                turn(squares[:, v, :], pa_sq[:, v // 2, cols], True, False)
                turn(squares[:, v, :], pb_sq[:, v // 2, cols], False, True)
            roots_turned = sb.tile([P, PACK, P], F32, name=f"roots_turned{pair}", tag=f"roots_turned{pair}")
            nc.scalar.activation(roots_turned[:], squares[:], ACT.Sqrt, bias=0.25)
            roots = bank((7, 4)[pair])
            for v in range(PACK):
                turn(roots[:, v, :], roots_turned[:, v, :], True, True)
            for u in range(2):
                t = 2 * pair + u
                ra_t = sb.tile([P, 2, P], F32, name=f"ra{t}", tag=f"ra{t}", align_bytes=64)
                nc.scalar.copy(ra_t[:], roots[:, 2 * u : 2 * u + 2, :])
                ra.append(ra_t)

        dt_tags = ("pa_sq0", "pb_sq0", "roots_turned0", "pa_sq1")
        dt = [sb.tile([P, S], F32, name=f"dt{t}", tag=dt_tags[t]) for t in range(PACK)]
        for t in range(PACK):
            nc.vector.tensor_tensor(dt[t][:].indirect(l2[:]), pb[:, t, :], pa_half[:, t, :], ALU.add)

        z_planes = sb.tile([P, PACK, S], BF16, name="z_planes", tag="z_planes")
        for t in range(PACK):
            nc.vector.tensor_copy(dt[t][:].indirect(l1[:]), ra[t][:].rearrange("p a b -> p (a b)"))
            nc.scalar.activation(z_planes[:, t, :], dt[t][:], ACT.Copy, scale=gain[:, t : t + 1])
        w2s = sb.tile([P, PACK, P], U8, name="w2s", tag="ra0", align_bytes=64)
        deal(w2s, w2s_raw, 1, slice(0, PACK))
        zq = sb.tile([P, PACK * S], BF16, name="zq", align_bytes=64)
        interleave(nc.scalar.copy, zq[:], z_planes[:])
        zw = sb.tile([P, S], U32, name="zw", align_bytes=64)
        zs = sb.tile([P, S], U8, name="zs", align_bytes=64)
        nc.vector.quantize_mx(out=zw[:].bitcast(FP8X4), scales=zs[:], in_=zq[:])
        for t in range(PACK):
            product(w2w, w2s, t, zw, zs, 0, S, h[t], f"bank{TURNED + t}")

        totals = {(t, b0): bank(sum_bank) for t in range(TURNED) for b0, b1, sum_bank, back_bank in SPANS[t]}

        def add_turned(t, b0, b1, src, start, stop):
            for b in range(b0, b1):
                turn(totals[t, b0][:, b, :], src[:, b * P : (b + 1) * P], start and b == b0, stop and b == b1 - 1)

        y6 = sb.tile([P, TURNED, S], F32, name="y6", tag="ra2", align_bytes=64)
        diff = sb.tile([P, TURNED, S], F32, name="diff", tag="z_planes")
        for t in range(TURNED):
            nc.vector.tensor_copy(y6[:, t], y[t][:].indirect(l6[:]))
            for b0, b1, sum_bank, back_bank in SPANS[t]:
                add_turned(t, b0, b1, y6[:, t], True, False)
        for t in range(TURNED):
            nc.vector.tensor_tensor(diff[:, t], y[t][:].indirect(l5[:]), y6[:, t], ALU.subtract)

        res = [sb.tile([P, PACK, c1 - c0], F32, name=f"res{c0}") for c0, c1 in PIECES]
        part = sb.tile([P, TURNED, S], F32, name="part")

        def fetch_part(t):
            nc.vector.tensor_tensor(part[:, t], h[t][:].indirect(l3[:]), diff[:, t], ALU.add)
            for b0, b1, sum_bank, back_bank in SPANS[t]:
                add_turned(t, b0, b1, part[:, t], False, False)

        def fetch_excess(t):
            nc.vector.tensor_tensor(diff[:, t], h[t][:].indirect(l4[:]), part[:, t], ALU.subtract)
            over = sb.tile([P, S], F32, name=f"over{t}")
            for b0, b1, sum_bank, back_bank in SPANS[t]:
                nc.scalar.activation(over[:, b0 * P : b1 * P], diff[:, t, b0 * P : b1 * P], ACT.Relu)
                add_turned(t, b0, b1, over[:], False, True)

        backs = {}

        def turn_back(t):
            larger = sb.tile([P, BLOCKS, P], F32, name=f"larger{t}")
            for b0, b1, sum_bank, back_bank in SPANS[t]:
                nc.scalar.copy(larger[:, b0:b1], totals[t, b0][:, b0:b1])
                back = bank(back_bank)
                for b in range(b0, b1):
                    turn(back[:, b, :], larger[:, b, :], True, True)
                    backs[t, b] = back

        for group in ((0, 1), (2,)):
            for step in (fetch_part, fetch_excess, turn_back):
                for t in group:
                    step(t)
        for piece, (c0, c1) in zip(res, PIECES):
            for t in range(TURNED):
                nc.scalar.copy(piece[:, t, :], backs[t, c0 // P][:].rearrange("p b j -> p (b j)")[:, c0:c1])

        ow = sb.tile([P, S], I32, name="ow", align_bytes=64)
        osc = sb.tile([P, S], U8, name="osc", align_bytes=64)
        out_rows = out_0.rearrange("(p t) j -> p t j", t=PACK)
        out_words = out_1[0].rearrange("p c r -> p (c r)").bitcast(I32)

        y_last = sb.tile([P, 2, S], F32, name="y_last", tag=f"h{TURNED - 1}")
        nc.vector.tensor_copy(y_last[:, 0], y[LAST][:].indirect(l5[:]))
        nc.vector.tensor_copy(y_last[:, 1], y[LAST][:].indirect(l6[:]))
        for piece, (c0, c1) in zip(res, PIECES):
            list_cols = slice(c0 // PER_COL, c1 // PER_COL)
            sums = sb.tile([P, 2, c1 - c0], F32, name=f"sums{c0}")
            nc.vector.tensor_tensor(sums[:, 0], h[LAST][:].indirect(l3[:, list_cols]), y_last[:, 0, c0:c1], ALU.add)
            nc.vector.tensor_tensor(sums[:, 1], h[LAST][:].indirect(l4[:, list_cols]), y_last[:, 1, c0:c1], ALU.add)
            nc.vector.tensor_tensor(piece[:, LAST], sums[:, 0], sums[:, 1], ALU.max)
            nc.sync.dma_start(out_rows[:, :, c0:c1], piece[:])
        for piece, (c0, c1) in zip(res, PIECES):
            is_last = c1 == S
            rounded = sb.tile(
                [P, PACK * (c1 - c0)], BF16, name=f"rounded{c0}", tag=f"rounded{0 if is_last else c0}", align_bytes=64
            )
            interleave(nc.vector.tensor_copy if is_last else nc.scalar.copy, rounded[:], piece[:])
            nc.vector.quantize_mx(out=ow[:, c0:c1].bitcast(FP8X4), scales=osc[:, c0:c1], in_=rounded[:])
            if c0 > 0:
                w0 = c0 if is_last else 0
                nc.sync.dma_start(out_words[:, w0:c1], ow[:, w0:c1])
        for q in range(QUADS):
            queue = nc.scalar if q % 2 else nc.sync
            queue.dma_start(out_2[0, 4 * q : 4 * q + 4, :].bitcast(I32), osc[32 * q : 32 * q + 4, :].bitcast(I32))
